import numpy as np
import ml_dtypes


def mxq(x, axis, fmt="e4m3"):
    dtype, down = {"e4m3": (ml_dtypes.float8_e4m3fn, 7), "e5m2": (ml_dtypes.float8_e5m2, 14)}[fmt]
    v = np.moveaxis(np.asarray(x, np.float32).astype(ml_dtypes.bfloat16).astype(np.float64), axis, -1)
    blocks = v.reshape(v.shape[:-1] + (-1, 32))
    amax = np.abs(blocks).max(-1, keepdims=True)
    byte = np.maximum(np.where(amax > 0, np.frexp(amax)[1] - 1 + 127, 0) - down, 1)
    scale = np.exp2(byte - 127.0)
    codes = (blocks / scale).astype(np.float32).astype(dtype).astype(np.float64)
    return np.moveaxis((codes * scale).reshape(v.shape), -1, axis)


WIDE = False


def mx_kscale(k):
    if not WIDE:
        return np.ones(k)
    levels = np.array([10, -10, 5, -5, 0])
    if k % 512:
        return np.exp2(np.random.permutation(np.resize(levels, k // 32))).repeat(32)
    a = np.empty((k // 512, 16))
    for p in range(k // 512):
        a[p, :8] = np.random.permutation(np.resize(levels, 8))
        for g in range(8):
            far = levels[np.abs(levels - a[p, g]) >= 10]
            a[p, g + 8] = far[np.random.randint(len(far))]
    return np.exp2(a.ravel()).repeat(32)


def f64(x):
    return np.asarray(x).astype(np.float64)


def striped8(idx):
    return np.asarray(idx).reshape(8, -1, 16).transpose(0, 2, 1).reshape(128, -1).astype(np.uint16)


def unstriped8(offs):
    return offs.reshape(8, 16, -1).transpose(0, 2, 1).reshape(8, -1).astype(np.int64)


def pick8(x, idx, run):
    r = np.arange(len(x))
    return x[r[:, None], idx[r % (8 * run) // run]]


E2M1 = np.array([0.0, 0.5, 1.0, 1.5, 2.0, 3.0, 4.0, 6.0, -0.0, -0.5, -1.0, -1.5, -2.0, -3.0, -4.0, -6.0])


def pack_weight(w, fmt):
    k, n = w.shape
    w = f64(np.asarray(w, np.float32).astype(ml_dtypes.bfloat16)).reshape(k // 32, 32, n)
    amax = np.abs(w).max(1)
    if fmt == "e4m3":
        byte = np.frexp(amax)[1] - 1 + 127 - 7
    else:
        mant, ex = np.frexp(amax / 6.0)
        byte = np.where(mant > 0.5, ex, ex - 1) + 127
    byte = np.clip(np.where(amax > 0, byte, 1), 1, 254)
    scaled = (w * np.exp2(127.0 - byte)[:, None, :]).reshape(k, n).astype(np.float32)
    by_word = np.ascontiguousarray(scaled.reshape(k // 512, 128, 4, n).transpose(0, 1, 3, 2))
    if fmt == "e4m3":
        words = by_word.astype(ml_dtypes.float8_e4m3fn).view(np.uint8)
    else:
        c = by_word.astype(ml_dtypes.float4_e2m1fn).view(np.uint8) & 0xF
        words = (c[..., 0::2] | (c[..., 1::2] << 4)).reshape(k // 512, 128, 2 * n)
    return np.ascontiguousarray(words), np.ascontiguousarray(byte.astype(np.uint8).reshape(k // 512, 16, n))


def unpack_weight(words, scales, fmt):
    g, _, n = scales.shape
    words = np.ascontiguousarray(words).reshape(g, 128, n, -1)
    if fmt == "e4m3":
        vals = words.view(ml_dtypes.float8_e4m3fn).astype(np.float64)
    else:
        nib = np.empty((g, 128, n, 4), np.uint8)
        nib[..., 0::2] = words & 0xF
        nib[..., 1::2] = words >> 4
        vals = E2M1[nib]
    vals = vals * np.repeat(np.exp2(scales.astype(np.float64) - 127.0), 8, axis=1)[..., None]
    return vals.transpose(0, 1, 3, 2).reshape(g * 512, n)


D, V, Q, I, G = 512, 2048, 128, 512, 64


def setup_inputs():
    n = np.random.standard_normal
    idx = np.stack([np.random.permutation(V)[:I] for _ in range(8)])
    fd = mx_kscale(D)
    vocp = pack_weight(n((D, V)) / fd[:, None], "e4m3")
    return {
        "hid": (n((D, Q)) * 1.0 / np.sqrt(D) * fd[:, None]).astype(np.float32),
        "voc_words": vocp[0],
        "voc_scales": vocp[1],
        "target": (np.random.uniform(0.0, 0.1, (Q, G))).astype(np.float32),
        "dhid": (n((D, Q)) * 1.0 / np.sqrt(D) * fd[:, None]).astype(np.float32),
        "base": (0.5 * n((Q, V))).astype(np.float32),
        "offs": striped8(idx),
    }


def reference(hid, voc_words, voc_scales, target, dhid, base, offs):
    idx = unstriped8(offs)
    vocu = unpack_weight(voc_words, voc_scales, "e4m3")
    hidq = mxq(f64(hid), 0, "e4m3")
    a = hidq.T @ vocu
    dhidq = mxq(f64(dhid), 0, "e4m3")
    ta = dhidq.T @ vocu
    m1 = np.max(a, axis=1, keepdims=True)
    p = np.exp(a - m1)
    z = np.sum(p, axis=1, keepdims=True)
    px = np.exp(pick8(a, idx, 16) - m1)
    u1 = px.reshape(Q, G, I // G).sum(axis=2) / z
    du1 = f64(target) / u1
    e1 = du1 / z
    r1 = np.repeat(e1, I // G, axis=1)
    dz = np.sum(du1 * px.reshape(Q, G, I // G).sum(axis=2) / np.square(z) * (-1.0), axis=1, keepdims=True)
    xp = ta * p
    xz = np.sum(xp, axis=1, keepdims=True)
    xpx = pick8(ta, idx, 16) * px
    xu1 = (xpx.reshape(Q, G, I // G).sum(axis=2) - xz * px.reshape(Q, G, I // G).sum(axis=2) / z) / z
    xdu1 = xu1 * f64(target) / np.square(u1) * (-1.0)
    xe1 = (xdu1 - xz * du1 / z) / z
    xr1 = np.repeat(xe1, I // G, axis=1)
    xdz = np.sum((xdu1 * px.reshape(Q, G, I // G).sum(axis=2) + xpx.reshape(Q, G, I // G).sum(axis=2) * du1 - xz * z * 2.0 * du1 * px.reshape(Q, G, I // G).sum(axis=2) / np.square(z)) / np.square(z) * (-1.0), axis=1, keepdims=True)
    xe2 = xr1 * px + xpx * r1
    xs2 = np.zeros((Q, V))
    xs2[np.arange(Q)[:, None], idx[np.arange(Q) % 128 // 16]] = xe2
    xda = xdz * p + xp * dz + xs2
    y = xda * 64.0 + f64(base)
    return y

@@ -1,0 +1,208 @@
+from contextlib import ExitStack
+
+import concourse.mybir as mybir
+from concourse.masks import make_identity
+
+D, V, Q, I, G = 512, 2048, 128, 512, 64
+FLOPS = 2 * 2 * D * Q * V
+
+F32 = mybir.dt.float32
+BF16 = mybir.dt.bfloat16
+I32 = mybir.dt.int32
+U32 = mybir.dt.uint32
+U16 = mybir.dt.uint16
+U8 = mybir.dt.uint8
+FP8X4 = mybir.dt.float8_e4m3fn_x4
+ALU = mybir.AluOpType
+ACT = mybir.ActivationFunctionType
+AX = mybir.AxisListType
+
+P = 128
+PACK = 4
+CH = 512
+NCH = V // CH
+GS = I // G
+NB = CH // P
+
+
+def tile_attend_hvgroupshare_heads_kernel(tc, hid, voc_words, voc_scales, target, dhid, base, offs, out):
+    nc = tc.nc
+    with ExitStack() as ctx:
+        sb = ctx.enter_context(tc.tile_pool(name="sb", bufs=1))
+        ps = ctx.enter_context(tc.psum_pool(name="ps", bufs=1))
+
+        offsets = sb.tile([P, I // 16], U16, name="offsets")
+        vsc = sb.tile([P, CH], U8, name="vsc", align_bytes=64)
+        words = [sb.tile([P, CH], U32, name="words%d" % k, align_bytes=64) for k in range(NCH)]
+        raw = [sb.tile([P, PACK, Q], F32, name="raw%d" % j) for j in range(2)]
+        grouped = [sb.tile([P, Q, PACK], BF16, name="grouped%d" % j, align_bytes=64) for j in range(2)]
+        codes = [sb.tile([P, Q], U32, name="codes%d" % j, align_bytes=64) for j in range(2)]
+        hsc = [sb.tile([P, Q], U8, name="hsc%d" % j, align_bytes=64) for j in range(2)]
+        tgt = sb.tile([P, G], F32, name="tgt")
+        base_sb = [sb.tile([P, CH], F32, name="base%d" % k) for k in range(NCH)]
+        a_sb = sb.tile([P, V], F32, name="a_sb")
+        ta_sb = sb.tile([P, V], F32, name="ta_sb")
+        xs = sb.tile([P, V], F32, name="xs")
+        ident = sb.tile([P, P], F32, name="ident")
+
+        nc.gpsimd.memset(vsc[:].bitcast(I32), 0)
+        nc.vector.memset(xs[:], 0.0)
+        make_identity(nc, ident[:])
+
+        scale_rows = voc_scales[0].bitcast(I32).rearrange("r (j c) -> j r c", j=NCH)
+        word_rows = voc_words[0].rearrange("p n t -> p (n t)").bitcast(I32)
+        nc.sync.dma_start(out=raw[0][:], in_=hid.rearrange("(p j) w -> p j w", j=PACK))
+        for qd in range(4):
+            nc.sync.dma_start(out=vsc[32 * qd : 32 * qd + 16, :].bitcast(I32), in_=scale_rows[:, 4 * qd : 4 * qd + 4, :])
+        nc.sync.dma_start(out=words[0][:].bitcast(I32), in_=word_rows[:, 0:CH])
+        nc.sync.dma_start(out=raw[1][:], in_=dhid.rearrange("(p j) w -> p j w", j=PACK))
+        for k in range(1, NCH):
+            nc.sync.dma_start(out=words[k][:].bitcast(I32), in_=word_rows[:, k * CH : (k + 1) * CH])
+        nc.sync.dma_start(offsets[:], offs)
+        nc.sync.dma_start(out=tgt[:], in_=target)
+        for k in range(NCH):
+            nc.sync.dma_start(out=base_sb[k][:], in_=base[:, k * CH : (k + 1) * CH])
+
+        for j in range(2):
+            nc.vector.tensor_copy(out=grouped[j][:], in_=raw[j][:].rearrange("p j w -> p w j"))
+            nc.vector.quantize_mx(out=codes[j][:].bitcast(FP8X4), scales=hsc[j][:], in_=grouped[j][:].rearrange("p w j -> p (w j)"))
+
+        def scores(j, k, bank):
+            nc.tensor.matmul_mx(out=bank[:], lhsT=codes[j][:].bitcast(FP8X4), lhsT_scale=hsc[j][:],
+                                rhs=words[k][:].bitcast(FP8X4), rhs_scale=vsc[4 * k : P, :], start=True, stop=True)
+
+        def cols(k):
+            return slice(k * CH, (k + 1) * CH)
+
+        a_ps = [ps.tile([P, CH], F32, name="a_ps%d" % k, tag="lo%d" % k) for k in range(NCH)]
+        t_ps = [ps.tile([P, CH], F32, name="t_ps%d" % k, tag="hi%d" % k) for k in range(NCH)]
+        for k in range(NCH):
+            scores(0, k, a_ps[k])
+        for k in range(NCH):
+            scores(1, k, t_ps[k])
+
+        mk = sb.tile([P, NCH], F32, name="mk")
+        nmk = sb.tile([P, NCH - 1], F32, name="nmk")
+        nm = sb.tile([P, 1], F32, name="nm")
+        fk = sb.tile([P, NCH], F32, name="fk")
+        zk = sb.tile([P, NCH], F32, name="zk")
+        yk = sb.tile([P, NCH], F32, name="yk")
+        p_sb = [sb.tile([P, CH], F32, name="p%d" % k) for k in range(NCH)]
+        xp = [sb.tile([P, CH], F32, name="xp%d" % k) for k in range(NCH)]
+        t64 = sb.tile([P, G], F32, name="t64")
+        nt = sb.tile([P, 1], F32, name="nt")
+        ag = sb.tile([P, I], F32, name="ag")
+        px = sb.tile([P, I], F32, name="px")
+        nc.gpsimd.memset(fk[:], 1.0)
+        for k in range(NCH):
+            nc.vector.tensor_scalar(out=a_sb[:, cols(k)], in0=a_ps[k][:], scalar1=1.0, scalar2=None, op0=ALU.mult, op1=ALU.max,
+                                    accum_out=mk[:, k : k + 1])
+            if k < NCH - 1:
+                nc.gpsimd.tensor_scalar(out=nmk[:, k : k + 1], in0=mk[:, k : k + 1], scalar1=-1.0, scalar2=0.0, op0=ALU.mult, op1=ALU.add)
+                shift = nmk[:, k : k + 1]
+            else:
+                nc.vector.tensor_reduce(out=nm[:], in_=mk[:], axis=AX.X, op=ALU.max, negate=True)
+                shift = nm[:]
+            nc.scalar.activation(out=p_sb[k][:], in_=a_sb[:, cols(k)], func=ACT.Exp, bias=shift, accum_out=zk[:, k : k + 1])
+        nc.vector.tensor_copy(out=ag[:], in_=a_sb[:].indirect(offsets[:]))
+        nc.scalar.activation(out=fk[:, 0 : NCH - 1], in_=mk[:, 0 : NCH - 1], func=ACT.Exp, bias=nm[:])
+
+        fz = sb.tile([P, NCH], F32, name="fz")
+        z = sb.tile([P, 1], F32, name="z")
+        rz = sb.tile([P, 1], F32, name="rz")
+        gk = sb.tile([P, NCH], F32, name="gk")
+        c1 = sb.tile([P, NCH], F32, name="c1")
+        ny = sb.tile([P, NCH], F32, name="ny")
+        mu = sb.tile([P, 1], F32, name="mu")
+        c2 = sb.tile([P, NCH], F32, name="c2")
+        sg = sb.tile([P, G], F32, name="sg")
+        rs = sb.tile([P, G], F32, name="rs")
+        eg = sb.tile([P, G], F32, name="eg")
+        w = sb.tile([P, I], F32, name="w")
+        xw = sb.tile([P, I], F32, name="xw")
+        nx = sb.tile([P, G], F32, name="nx")
+        kg = sb.tile([P, G], F32, name="kg")
+        pk = sb.tile([P, I], F32, name="pk")
+
+        def by_group(ap):
+            return ap.rearrange("p (g s) -> p g s", s=GS)
+
+        def spread(ap):
+            return ap.unsqueeze(2).to_broadcast([P, ap.shape[1], GS])
+
+        def copy_ta(k):
+            nc.scalar.copy(out=ta_sb[:, cols(k)], in_=t_ps[k][:])
+
+        def xp_pool(k):
+            nc.gpsimd.tensor_tensor(out=xp[k][:], in0=ta_sb[:, cols(k)], in1=p_sb[k][:], op=ALU.mult)
+
+        def xp_vec(k):
+            nc.vector.tensor_tensor(out=xp[k][:], in0=t_ps[k][:], in1=p_sb[k][:], op=ALU.mult)
+
+        HS, HG, HO = I // 2, G // 2, I // 32
+        halves = [(slice(h * HS, (h + 1) * HS), slice(h * HG, (h + 1) * HG), slice(h * HO, (h + 1) * HO)) for h in range(2)]
+        nc.scalar.activation(out=t64[:], in_=tgt[:], func=ACT.Copy, scale=-64.0, accum_out=nt[:])
+        copy_ta(0)
+        xp_pool(0)
+        nc.scalar.activation(out=px[:], in_=ag[:], func=ACT.Exp, bias=nm[:])
+        copy_ta(1)
+        xp_pool(1)
+        xp_vec(2)
+        copy_ta(2)
+        xp_vec(3)
+        copy_ta(3)
+        for sl, gr, oc in halves:
+            nc.vector.tensor_reduce(out=sg[:, gr], in_=by_group(px[:, sl]), axis=AX.X, op=ALU.add, negate=True)
+        for sl, gr, oc in halves:
+            nc.vector.reciprocal(out=rs[:, gr], in_=sg[:, gr])
+        nc.vector.tensor_tensor(out=eg[:, halves[0][1]], in0=t64[:, halves[0][1]], in1=rs[:, halves[0][1]], op=ALU.mult)
+        nc.vector.scalar_tensor_tensor(out=fz[:], in0=fk[:], scalar=1.0, in1=zk[:], op0=ALU.mult, op1=ALU.mult, accum_out=z[:])
+        nc.vector.tensor_tensor(out=eg[:, halves[1][1]], in0=t64[:, halves[1][1]], in1=rs[:, halves[1][1]], op=ALU.mult)
+        for sl, gr, oc in halves:
+            nc.vector.tensor_tensor(out=by_group(w[:, sl]), in0=by_group(px[:, sl]), in1=spread(eg[:, gr]), op=ALU.mult)
+            if sl.start == 0:
+                nc.vector.reciprocal(out=rz[:], in_=z[:])
+        HS, HG, HO = I // 2, G // 2, I // 32
+        halves = [(slice(h * HS, (h + 1) * HS), slice(h * HG, (h + 1) * HG), slice(h * HO, (h + 1) * HO)) for h in range(2)]
+        for sl, gr, oc in halves:
+            nc.vector.tensor_tensor(out=xw[:, sl], in0=ta_sb[:].indirect(offsets[:, oc]), in1=w[:, sl], op=ALU.mult)
+        for sl, gr, oc in halves:
+            nc.vector.tensor_reduce(out=nx[:, gr], in_=by_group(xw[:, sl]), axis=AX.X, op=ALU.add)
+        for sl, gr, oc in halves:
+            nc.vector.tensor_tensor(out=kg[:, gr], in0=nx[:, gr], in1=rs[:, gr], op=ALU.mult)
+        for sl, gr, oc in halves:
+            nc.vector.tensor_tensor(out=by_group(pk[:, sl]), in0=by_group(px[:, sl]), in1=spread(kg[:, gr]), op=ALU.mult)
+        nc.vector.tensor_tensor(out=xs[:].indirect(offsets[:]), in0=xw[:], in1=pk[:], op=ALU.add)
+
+        xq = [sb.tile([P, CH], F32, name="xq%d" % k) for k in range(NCH)]
+        pq = [sb.tile([P, CH], F32, name="pq%d" % k) for k in range(NCH)]
+        mid = [sb.tile([P, CH], F32, name="mid%d" % k) for k in range(NCH)]
+        res = [sb.tile([P, CH], F32, name="res%d" % k) for k in range(NCH)]
+        s_ps = [ps.tile([P, CH], F32, name="s_ps%d" % k, tag="lo%d" % k) for k in range(NCH)]
+        r_ps = [ps.tile([P, CH], F32, name="r_ps%d" % k, tag="hi%d" % k) for k in range(NCH)]
+
+        def turn(bank, src, first, last):
+            for b in range(NB):
+                blk = slice(b * P, (b + 1) * P)
+                nc.tensor.matmul(out=bank[:, blk], lhsT=src[:, blk], rhs=ident[:], is_transpose=True,
+                                 start=(first and b == 0), stop=(last and b == NB - 1))
+
+        for k in range(NCH):
+            turn(s_ps[k], base_sb[k], True, False)
+        nc.scalar.activation(out=gk[:], in_=fk[:], func=ACT.Copy, scale=rz[:])
+        nc.scalar.activation(out=c1[:], in_=gk[:], func=ACT.Copy, scale=nt[:])
+        for k in (2, 3, 0, 1):
+            nc.scalar.activation(out=xq[k][:], in_=xp[k][:], func=ACT.Copy, scale=c1[:, k : k + 1], accum_out=yk[:, k : k + 1])
+            turn(s_ps[k], xq[k], False, False)
+        nc.scalar.activation(out=ny[:], in_=yk[:], func=ACT.Copy, scale=-1.0, accum_out=mu[:])
+        nc.scalar.activation(out=c2[:], in_=gk[:], func=ACT.Copy, scale=mu[:])
+        for k in range(NCH + 1):
+            if k < NCH:
+                nc.scalar.activation(out=pq[k][:], in_=p_sb[k][:], func=ACT.Copy, scale=c2[:, k : k + 1])
+                turn(s_ps[k], pq[k], False, True)
+            if k > 0:
+                nc.scalar.copy(out=mid[k - 1][:], in_=s_ps[k - 1][:])
+                turn(r_ps[k - 1], mid[k - 1], True, True)
+        for k in range(NCH):
+            nc.vector.tensor_tensor(out=res[k][:], in0=r_ps[k][:], in1=xs[:, cols(k)], op=ALU.add)
+            nc.sync.dma_start(out=out[:, cols(k)], in_=res[k][:])

@@ -45,26 +45,36 @@ def tile_attend_hvgroupshare_heads_kernel(tc, hid, voc_words, voc_scales, target
         xs = sb.tile([P, V], F32, name="xs")
         ident = sb.tile([P, P], F32, name="ident")
 
-        nc.gpsimd.memset(vsc[:].bitcast(I32), 0)
+        nc.vector.memset(vsc[:].bitcast(I32), 0)
         nc.vector.memset(xs[:], 0.0)
         make_identity(nc, ident[:])
 
         scale_rows = voc_scales[0].bitcast(I32).rearrange("r (j c) -> j r c", j=NCH)
         word_rows = voc_words[0].rearrange("p n t -> p (n t)").bitcast(I32)
-        nc.sync.dma_start(out=raw[0][:], in_=hid.rearrange("(p j) w -> p j w", j=PACK))
-        for qd in range(4):
-            nc.sync.dma_start(out=vsc[32 * qd : 32 * qd + 16, :].bitcast(I32), in_=scale_rows[:, 4 * qd : 4 * qd + 4, :])
-        nc.sync.dma_start(out=words[0][:].bitcast(I32), in_=word_rows[:, 0:CH])
-        nc.sync.dma_start(out=raw[1][:], in_=dhid.rearrange("(p j) w -> p j w", j=PACK))
-        for k in range(1, NCH):
+        def load_scales(qd, queue):
+            queue.dma_start(out=vsc[32 * qd : 32 * qd + 16, :].bitcast(I32), in_=scale_rows[:, 4 * qd : 4 * qd + 4, :])
+
+        def load_words(k):
             nc.sync.dma_start(out=words[k][:].bitcast(I32), in_=word_rows[:, k * CH : (k + 1) * CH])
+
+        nc.sync.dma_start(out=raw[0][:], in_=hid.rearrange("(p j) w -> p j w", j=PACK))
+        load_scales(2, nc.scalar)
+        load_words(0)
+        load_scales(3, nc.scalar)
+        load_scales(0, nc.sync)
+        load_scales(1, nc.sync)
+        nc.sync.dma_start(out=raw[1][:], in_=dhid.rearrange("(p j) w -> p j w", j=PACK))
+        load_words(1)
+        load_words(2)
         nc.sync.dma_start(offsets[:], offs)
+        load_words(3)
         nc.sync.dma_start(out=tgt[:], in_=target)
         for k in range(NCH):
             nc.sync.dma_start(out=base_sb[k][:], in_=base[:, k * CH : (k + 1) * CH])
 
         for j in range(2):
-            nc.vector.tensor_copy(out=grouped[j][:], in_=raw[j][:].rearrange("p j w -> p w j"))
+            nc.vector.tensor_copy(out=grouped[j][:, 0 : Q // 2, :], in_=raw[j][:, :, 0 : Q // 2].rearrange("p j w -> p w j"))
+            nc.scalar.copy(out=grouped[j][:, Q // 2 : Q, :], in_=raw[j][:, :, Q // 2 : Q].rearrange("p j w -> p w j"))
             nc.vector.quantize_mx(out=codes[j][:].bitcast(FP8X4), scales=hsc[j][:], in_=grouped[j][:].rearrange("p w j -> p (w j)"))
 
         def scores(j, k, bank):
@@ -84,6 +94,8 @@ def tile_attend_hvgroupshare_heads_kernel(tc, hid, voc_words, voc_scales, target
         mk = sb.tile([P, NCH], F32, name="mk")
         nmk = sb.tile([P, NCH - 1], F32, name="nmk")
         nm = sb.tile([P, 1], F32, name="nm")
+        nm3 = sb.tile([P, 1], F32, name="nm3")
+        over = sb.tile([P, 1], F32, name="over")
         fk = sb.tile([P, NCH], F32, name="fk")
         zk = sb.tile([P, NCH], F32, name="zk")
         yk = sb.tile([P, NCH], F32, name="yk")
@@ -101,11 +113,13 @@ def tile_attend_hvgroupshare_heads_kernel(tc, hid, voc_words, voc_scales, target
                 nc.gpsimd.tensor_scalar(out=nmk[:, k : k + 1], in0=mk[:, k : k + 1], scalar1=-1.0, scalar2=0.0, op0=ALU.mult, op1=ALU.add)
                 shift = nmk[:, k : k + 1]
             else:
-                nc.vector.tensor_reduce(out=nm[:], in_=mk[:], axis=AX.X, op=ALU.max, negate=True)
+                nc.gpsimd.tensor_scalar(out=nm3[:], in0=nmk[:, 0:1], scalar1=nmk[:, 1:2], scalar2=nmk[:, 2:3], op0=ALU.min, op1=ALU.min)
+                nc.scalar.activation(out=over[:], in_=mk[:, k : k + 1], func=ACT.Relu, bias=nm3[:])
+                nc.scalar.activation(out=nm[:], in_=over[:], func=ACT.Identity, scale=-1.0, bias=nm3[:])
                 shift = nm[:]
+                nc.scalar.activation(out=fk[:, 0 : NCH - 1], in_=mk[:, 0 : NCH - 1], func=ACT.Exp, bias=nm[:])
             nc.scalar.activation(out=p_sb[k][:], in_=a_sb[:, cols(k)], func=ACT.Exp, bias=shift, accum_out=zk[:, k : k + 1])
         nc.vector.tensor_copy(out=ag[:], in_=a_sb[:].indirect(offsets[:]))
-        nc.scalar.activation(out=fk[:, 0 : NCH - 1], in_=mk[:, 0 : NCH - 1], func=ACT.Exp, bias=nm[:])
 
         fz = sb.tile([P, NCH], F32, name="fz")
         z = sb.tile([P, 1], F32, name="z")
@@ -136,6 +150,12 @@ def tile_attend_hvgroupshare_heads_kernel(tc, hid, voc_words, voc_scales, target
         def xp_pool(k):
             nc.gpsimd.tensor_tensor(out=xp[k][:], in0=ta_sb[:, cols(k)], in1=p_sb[k][:], op=ALU.mult)
 
+        xq = [sb.tile([P, CH], F32, name="xq%d" % k) for k in range(NCH)]
+
+        def xq_vec(k):
+            nc.vector.scalar_tensor_tensor(out=xq[k][:], in0=t_ps[k][:], scalar=c1[:, k : k + 1], in1=p_sb[k][:], op0=ALU.mult, op1=ALU.mult,
+                                           accum_out=yk[:, k : k + 1])
+
         def xp_vec(k):
             nc.vector.tensor_tensor(out=xp[k][:], in0=t_ps[k][:], in1=p_sb[k][:], op=ALU.mult)
 
@@ -144,24 +164,25 @@ def tile_attend_hvgroupshare_heads_kernel(tc, hid, voc_words, voc_scales, target
         nc.scalar.activation(out=t64[:], in_=tgt[:], func=ACT.Copy, scale=-64.0, accum_out=nt[:])
         copy_ta(0)
         xp_pool(0)
+        nc.vector.scalar_tensor_tensor(out=fz[:], in0=fk[:], scalar=1.0, in1=zk[:], op0=ALU.mult, op1=ALU.mult, accum_out=z[:])
         nc.scalar.activation(out=px[:], in_=ag[:], func=ACT.Exp, bias=nm[:])
         copy_ta(1)
         xp_pool(1)
         xp_vec(2)
+        nc.vector.reciprocal(out=rz[:], in_=z[:])
         copy_ta(2)
-        xp_vec(3)
+        nc.scalar.activation(out=gk[:], in_=fk[:], func=ACT.Copy, scale=rz[:])
+        nc.vector.tensor_reduce(out=sg[:, halves[0][1]], in_=by_group(px[:, halves[0][0]]), axis=AX.X, op=ALU.add, negate=True)
+        nc.vector.tensor_scalar(out=c1[:], in0=fk[:], scalar1=rz[:], scalar2=nt[:], op0=ALU.mult, op1=ALU.mult)
+        nc.vector.tensor_reduce(out=sg[:, halves[1][1]], in_=by_group(px[:, halves[1][0]]), axis=AX.X, op=ALU.add, negate=True)
+        xq_vec(3)
         copy_ta(3)
         for sl, gr, oc in halves:
-            nc.vector.tensor_reduce(out=sg[:, gr], in_=by_group(px[:, sl]), axis=AX.X, op=ALU.add, negate=True)
-        for sl, gr, oc in halves:
             nc.vector.reciprocal(out=rs[:, gr], in_=sg[:, gr])
-        nc.vector.tensor_tensor(out=eg[:, halves[0][1]], in0=t64[:, halves[0][1]], in1=rs[:, halves[0][1]], op=ALU.mult)
-        nc.vector.scalar_tensor_tensor(out=fz[:], in0=fk[:], scalar=1.0, in1=zk[:], op0=ALU.mult, op1=ALU.mult, accum_out=z[:])
-        nc.vector.tensor_tensor(out=eg[:, halves[1][1]], in0=t64[:, halves[1][1]], in1=rs[:, halves[1][1]], op=ALU.mult)
+        for sl, gr, oc in halves:
+            nc.vector.tensor_tensor(out=eg[:, gr], in0=t64[:, gr], in1=rs[:, gr], op=ALU.mult)
         for sl, gr, oc in halves:
             nc.vector.tensor_tensor(out=by_group(w[:, sl]), in0=by_group(px[:, sl]), in1=spread(eg[:, gr]), op=ALU.mult)
-            if sl.start == 0:
-                nc.vector.reciprocal(out=rz[:], in_=z[:])
         HS, HG, HO = I // 2, G // 2, I // 32
         halves = [(slice(h * HS, (h + 1) * HS), slice(h * HG, (h + 1) * HG), slice(h * HO, (h + 1) * HO)) for h in range(2)]
         for sl, gr, oc in halves:
@@ -174,7 +195,6 @@ def tile_attend_hvgroupshare_heads_kernel(tc, hid, voc_words, voc_scales, target
             nc.vector.tensor_tensor(out=by_group(pk[:, sl]), in0=by_group(px[:, sl]), in1=spread(kg[:, gr]), op=ALU.mult)
         nc.vector.tensor_tensor(out=xs[:].indirect(offsets[:]), in0=xw[:], in1=pk[:], op=ALU.add)
 
-        xq = [sb.tile([P, CH], F32, name="xq%d" % k) for k in range(NCH)]
         pq = [sb.tile([P, CH], F32, name="pq%d" % k) for k in range(NCH)]
         mid = [sb.tile([P, CH], F32, name="mid%d" % k) for k in range(NCH)]
         res = [sb.tile([P, CH], F32, name="res%d" % k) for k in range(NCH)]
@@ -189,20 +209,23 @@ def tile_attend_hvgroupshare_heads_kernel(tc, hid, voc_words, voc_scales, target
 
         for k in range(NCH):
             turn(s_ps[k], base_sb[k], True, False)
-        nc.scalar.activation(out=gk[:], in_=fk[:], func=ACT.Copy, scale=rz[:])
-        nc.scalar.activation(out=c1[:], in_=gk[:], func=ACT.Copy, scale=nt[:])
-        for k in (2, 3, 0, 1):
+        for k in (3,):
+            turn(s_ps[k], xq[k], False, False)
+        for k in (2, 0, 1):
             nc.scalar.activation(out=xq[k][:], in_=xp[k][:], func=ACT.Copy, scale=c1[:, k : k + 1], accum_out=yk[:, k : k + 1])
             turn(s_ps[k], xq[k], False, False)
         nc.scalar.activation(out=ny[:], in_=yk[:], func=ACT.Copy, scale=-1.0, accum_out=mu[:])
         nc.scalar.activation(out=c2[:], in_=gk[:], func=ACT.Copy, scale=mu[:])
-        for k in range(NCH + 1):
+        for k in range(NCH + 2):
             if k < NCH:
                 nc.scalar.activation(out=pq[k][:], in_=p_sb[k][:], func=ACT.Copy, scale=c2[:, k : k + 1])
                 turn(s_ps[k], pq[k], False, True)
-            if k > 0:
-                nc.scalar.copy(out=mid[k - 1][:], in_=s_ps[k - 1][:])
-                turn(r_ps[k - 1], mid[k - 1], True, True)
-        for k in range(NCH):
-            nc.vector.tensor_tensor(out=res[k][:], in0=r_ps[k][:], in1=xs[:, cols(k)], op=ALU.add)
-            nc.sync.dma_start(out=out[:, cols(k)], in_=res[k][:])
+            if k > 1:
+                nc.scalar.copy(out=mid[k - 2][:], in_=s_ps[k - 2][:])
+                turn(r_ps[k - 2], mid[k - 2], True, True)
+        c0 = 0
+        for width in (256, 256, 512, 512, 512):
+            k, lo = divmod(c0, CH)
+            nc.vector.tensor_tensor(out=res[k][:, lo : lo + width], in0=r_ps[k][:, lo : lo + width], in1=xs[:, c0 : c0 + width], op=ALU.add)
+            nc.sync.dma_start(out=out[:, c0 : c0 + width], in_=res[k][:, lo : lo + width])
+            c0 = c0 + width

@@ -73,8 +73,7 @@ def tile_attend_hvgroupshare_heads_kernel(tc, hid, voc_words, voc_scales, target
             nc.sync.dma_start(out=base_sb[k][:], in_=base[:, k * CH : (k + 1) * CH])
 
         for j in range(2):
-            nc.vector.tensor_copy(out=grouped[j][:, 0 : Q // 2, :], in_=raw[j][:, :, 0 : Q // 2].rearrange("p j w -> p w j"))
-            nc.scalar.copy(out=grouped[j][:, Q // 2 : Q, :], in_=raw[j][:, :, Q // 2 : Q].rearrange("p j w -> p w j"))
+            nc.vector.tensor_copy(out=grouped[j][:], in_=raw[j][:].rearrange("p j w -> p w j"))
             nc.vector.quantize_mx(out=codes[j][:].bitcast(FP8X4), scales=hsc[j][:], in_=grouped[j][:].rearrange("p w j -> p (w j)"))
 
         def scores(j, k, bank):
@@ -94,8 +93,6 @@ def tile_attend_hvgroupshare_heads_kernel(tc, hid, voc_words, voc_scales, target
         mk = sb.tile([P, NCH], F32, name="mk")
         nmk = sb.tile([P, NCH - 1], F32, name="nmk")
         nm = sb.tile([P, 1], F32, name="nm")
-        nm3 = sb.tile([P, 1], F32, name="nm3")
-        over = sb.tile([P, 1], F32, name="over")
         fk = sb.tile([P, NCH], F32, name="fk")
         zk = sb.tile([P, NCH], F32, name="zk")
         yk = sb.tile([P, NCH], F32, name="yk")
@@ -113,15 +110,12 @@ def tile_attend_hvgroupshare_heads_kernel(tc, hid, voc_words, voc_scales, target
                 nc.gpsimd.tensor_scalar(out=nmk[:, k : k + 1], in0=mk[:, k : k + 1], scalar1=-1.0, scalar2=0.0, op0=ALU.mult, op1=ALU.add)
                 shift = nmk[:, k : k + 1]
             else:
-                nc.gpsimd.tensor_scalar(out=nm3[:], in0=nmk[:, 0:1], scalar1=nmk[:, 1:2], scalar2=nmk[:, 2:3], op0=ALU.min, op1=ALU.min)
-                nc.scalar.activation(out=over[:], in_=mk[:, k : k + 1], func=ACT.Relu, bias=nm3[:])
-                nc.scalar.activation(out=nm[:], in_=over[:], func=ACT.Identity, scale=-1.0, bias=nm3[:])
+                nc.vector.tensor_reduce(out=nm[:], in_=mk[:], axis=AX.X, op=ALU.max, negate=True)
                 shift = nm[:]
                 nc.scalar.activation(out=fk[:, 0 : NCH - 1], in_=mk[:, 0 : NCH - 1], func=ACT.Exp, bias=nm[:])
             nc.scalar.activation(out=p_sb[k][:], in_=a_sb[:, cols(k)], func=ACT.Exp, bias=shift, accum_out=zk[:, k : k + 1])
         nc.vector.tensor_copy(out=ag[:], in_=a_sb[:].indirect(offsets[:]))
 
-        fz = sb.tile([P, NCH], F32, name="fz")
         z = sb.tile([P, 1], F32, name="z")
         rz = sb.tile([P, 1], F32, name="rz")
         gk = sb.tile([P, NCH], F32, name="gk")
@@ -162,23 +156,23 @@ def tile_attend_hvgroupshare_heads_kernel(tc, hid, voc_words, voc_scales, target
         HS, HG, HO = I // 2, G // 2, I // 32
         halves = [(slice(h * HS, (h + 1) * HS), slice(h * HG, (h + 1) * HG), slice(h * HO, (h + 1) * HO)) for h in range(2)]
         nc.scalar.activation(out=t64[:], in_=tgt[:], func=ACT.Copy, scale=-64.0, accum_out=nt[:])
+        nc.vector.scalar_tensor_tensor(out=xp[0][:, 0:NCH], in0=fk[:], scalar=1.0, in1=zk[:], op0=ALU.mult, op1=ALU.mult, accum_out=z[:])
         copy_ta(0)
         xp_pool(0)
-        nc.vector.scalar_tensor_tensor(out=fz[:], in0=fk[:], scalar=1.0, in1=zk[:], op0=ALU.mult, op1=ALU.mult, accum_out=z[:])
         nc.scalar.activation(out=px[:], in_=ag[:], func=ACT.Exp, bias=nm[:])
-        copy_ta(1)
-        xp_pool(1)
         xp_vec(2)
         nc.vector.reciprocal(out=rz[:], in_=z[:])
-        copy_ta(2)
         nc.scalar.activation(out=gk[:], in_=fk[:], func=ACT.Copy, scale=rz[:])
-        nc.vector.tensor_reduce(out=sg[:, halves[0][1]], in_=by_group(px[:, halves[0][0]]), axis=AX.X, op=ALU.add, negate=True)
-        nc.vector.tensor_scalar(out=c1[:], in0=fk[:], scalar1=rz[:], scalar2=nt[:], op0=ALU.mult, op1=ALU.mult)
-        nc.vector.tensor_reduce(out=sg[:, halves[1][1]], in_=by_group(px[:, halves[1][0]]), axis=AX.X, op=ALU.add, negate=True)
-        xq_vec(3)
-        copy_ta(3)
+        copy_ta(1)
+        xp_pool(1)
+        nc.scalar.activation(out=c1[:], in_=gk[:], func=ACT.Copy, scale=nt[:])
+        copy_ta(2)
+        for sl, gr, oc in halves:
+            nc.vector.tensor_reduce(out=sg[:, gr], in_=by_group(px[:, sl]), axis=AX.X, op=ALU.add, negate=True)
         for sl, gr, oc in halves:
             nc.vector.reciprocal(out=rs[:, gr], in_=sg[:, gr])
+        xq_vec(3)
+        copy_ta(3)
         for sl, gr, oc in halves:
             nc.vector.tensor_tensor(out=eg[:, gr], in0=t64[:, gr], in1=rs[:, gr], op=ALU.mult)
         for sl, gr, oc in halves:

@@ -23,6 +23,7 @@ CH = 512
 NCH = V // CH
 GS = I // G
 NB = CH // P
+EARLY = 2
 
 
 def tile_attend_hvgroupshare_heads_kernel(tc, hid, voc_words, voc_scales, target, dhid, base, offs, out):
@@ -35,12 +36,11 @@ def tile_attend_hvgroupshare_heads_kernel(tc, hid, voc_words, voc_scales, target
         vsc = sb.tile([P, CH], U8, name="vsc", align_bytes=64)
         words = [sb.tile([P, CH], U32, name="words%d" % k, align_bytes=64) for k in range(NCH)]
         raw = [sb.tile([P, PACK, Q], F32, name="raw%d" % j) for j in range(2)]
-        grouped = [sb.tile([P, Q, PACK], BF16, name="grouped%d" % j, align_bytes=64) for j in range(2)]
+        grouped = [sb.tile([P, Q, PACK], BF16, name="grouped%d" % j, tag="grouped%d" % j, align_bytes=64) for j in range(2)]
         codes = [sb.tile([P, Q], U32, name="codes%d" % j, align_bytes=64) for j in range(2)]
         hsc = [sb.tile([P, Q], U8, name="hsc%d" % j, align_bytes=64) for j in range(2)]
         tgt = sb.tile([P, G], F32, name="tgt")
         base_sb = [sb.tile([P, CH], F32, name="base%d" % k) for k in range(NCH)]
-        a_sb = sb.tile([P, V], F32, name="a_sb")
         ta_sb = sb.tile([P, V], F32, name="ta_sb")
         xs = sb.tile([P, V], F32, name="xs")
         ident = sb.tile([P, P], F32, name="ident")
@@ -54,8 +54,8 @@ def tile_attend_hvgroupshare_heads_kernel(tc, hid, voc_words, voc_scales, target
         def load_scales(qd, queue):
             queue.dma_start(out=vsc[32 * qd : 32 * qd + 16, :].bitcast(I32), in_=scale_rows[:, 4 * qd : 4 * qd + 4, :])
 
-        def load_words(k):
-            nc.sync.dma_start(out=words[k][:].bitcast(I32), in_=word_rows[:, k * CH : (k + 1) * CH])
+        def load_words(k, queue=nc.sync):
+            queue.dma_start(out=words[k][:].bitcast(I32), in_=word_rows[:, k * CH : (k + 1) * CH])
 
         nc.sync.dma_start(out=raw[0][:], in_=hid.rearrange("(p j) w -> p j w", j=PACK))
         load_scales(2, nc.scalar)
@@ -66,8 +66,8 @@ def tile_attend_hvgroupshare_heads_kernel(tc, hid, voc_words, voc_scales, target
         nc.sync.dma_start(out=raw[1][:], in_=dhid.rearrange("(p j) w -> p j w", j=PACK))
         load_words(1)
         load_words(2)
-        nc.sync.dma_start(offsets[:], offs)
         load_words(3)
+        nc.sync.dma_start(offsets[:], offs)
         nc.sync.dma_start(out=tgt[:], in_=target)
         for k in range(NCH):
             nc.sync.dma_start(out=base_sb[k][:], in_=base[:, k * CH : (k + 1) * CH])
@@ -84,17 +84,15 @@ def tile_attend_hvgroupshare_heads_kernel(tc, hid, voc_words, voc_scales, target
             return slice(k * CH, (k + 1) * CH)
 
         a_ps = [ps.tile([P, CH], F32, name="a_ps%d" % k, tag="lo%d" % k) for k in range(NCH)]
-        t_ps = [ps.tile([P, CH], F32, name="t_ps%d" % k, tag="hi%d" % k) for k in range(NCH)]
         for k in range(NCH):
             scores(0, k, a_ps[k])
-        for k in range(NCH):
-            scores(1, k, t_ps[k])
 
+        a_sb = sb.tile([P, V], F32, name="a_sb", tag="grouped1", align_bytes=64)
         mk = sb.tile([P, NCH], F32, name="mk")
-        nmk = sb.tile([P, NCH - 1], F32, name="nmk")
+        nmk = sb.tile([P, EARLY], F32, name="nmk")
         nm = sb.tile([P, 1], F32, name="nm")
         fk = sb.tile([P, NCH], F32, name="fk")
-        zk = sb.tile([P, NCH], F32, name="zk")
+        zk = sb.tile([P, NCH + EARLY], F32, name="zk")
         yk = sb.tile([P, NCH], F32, name="yk")
         p_sb = [sb.tile([P, CH], F32, name="p%d" % k) for k in range(NCH)]
         xp = [sb.tile([P, CH], F32, name="xp%d" % k) for k in range(NCH)]
@@ -103,18 +101,35 @@ def tile_attend_hvgroupshare_heads_kernel(tc, hid, voc_words, voc_scales, target
         ag = sb.tile([P, I], F32, name="ag")
         px = sb.tile([P, I], F32, name="px")
         nc.gpsimd.memset(fk[:], 1.0)
+
+        def exp_chunk(k, shift):
+            nc.scalar.activation(out=p_sb[k][:], in_=a_sb[:, cols(k)], func=ACT.Exp, bias=shift, accum_out=zk[:, k : k + 1])
+
+        def copy_ta(k):
+            nc.scalar.copy(out=ta_sb[:, cols(k)], in_=t_ps[k][:])
+
         for k in range(NCH):
             nc.vector.tensor_scalar(out=a_sb[:, cols(k)], in0=a_ps[k][:], scalar1=1.0, scalar2=None, op0=ALU.mult, op1=ALU.max,
                                     accum_out=mk[:, k : k + 1])
-            if k < NCH - 1:
-                nc.gpsimd.tensor_scalar(out=nmk[:, k : k + 1], in0=mk[:, k : k + 1], scalar1=-1.0, scalar2=0.0, op0=ALU.mult, op1=ALU.add)
-                shift = nmk[:, k : k + 1]
-            else:
-                nc.vector.tensor_reduce(out=nm[:], in_=mk[:], axis=AX.X, op=ALU.max, negate=True)
-                shift = nm[:]
-                nc.scalar.activation(out=fk[:, 0 : NCH - 1], in_=mk[:, 0 : NCH - 1], func=ACT.Exp, bias=nm[:])
-            nc.scalar.activation(out=p_sb[k][:], in_=a_sb[:, cols(k)], func=ACT.Exp, bias=shift, accum_out=zk[:, k : k + 1])
+            if k < EARLY:
+                nc.scalar.activation(out=nmk[:, k : k + 1], in_=mk[:, k : k + 1], func=ACT.Copy, scale=-1.0)
+                exp_chunk(k, nmk[:, k : k + 1])
+        nc.vector.tensor_reduce(out=nm[:], in_=mk[:], axis=AX.X, op=ALU.max, negate=True)
+        t_ps = {}
+
+        def tangent(k, tag):
+            t_ps[k] = ps.tile([P, CH], F32, name="t_ps%d" % k, tag=tag)
+            scores(1, k, t_ps[k])
+
+        tangent(3, "lo0")
+        tangent(0, "lo2")
+        tangent(1, "lo3")
+        nc.scalar.activation(out=t64[:], in_=tgt[:], func=ACT.Copy, scale=-64.0, accum_out=nt[:])
+        copy_ta(3)
+        tangent(2, "lo0")
         nc.vector.tensor_copy(out=ag[:], in_=a_sb[:].indirect(offsets[:]))
+        nc.scalar.activation(out=fk[:, 0:EARLY], in_=mk[:, 0:EARLY], func=ACT.Exp, bias=nm[:])
+        exp_chunk(3, nm[:])
 
         z = sb.tile([P, 1], F32, name="z")
         rz = sb.tile([P, 1], F32, name="rz")
@@ -138,9 +153,6 @@ def tile_attend_hvgroupshare_heads_kernel(tc, hid, voc_words, voc_scales, target
         def spread(ap):
             return ap.unsqueeze(2).to_broadcast([P, ap.shape[1], GS])
 
-        def copy_ta(k):
-            nc.scalar.copy(out=ta_sb[:, cols(k)], in_=t_ps[k][:])
-
         def xp_pool(k):
             nc.gpsimd.tensor_tensor(out=xp[k][:], in0=ta_sb[:, cols(k)], in1=p_sb[k][:], op=ALU.mult)
 
@@ -155,28 +167,29 @@ def tile_attend_hvgroupshare_heads_kernel(tc, hid, voc_words, voc_scales, target
 
         HS, HG, HO = I // 2, G // 2, I // 32
         halves = [(slice(h * HS, (h + 1) * HS), slice(h * HG, (h + 1) * HG), slice(h * HO, (h + 1) * HO)) for h in range(2)]
-        nc.scalar.activation(out=t64[:], in_=tgt[:], func=ACT.Copy, scale=-64.0, accum_out=nt[:])
-        nc.vector.scalar_tensor_tensor(out=xp[0][:, 0:NCH], in0=fk[:], scalar=1.0, in1=zk[:], op0=ALU.mult, op1=ALU.mult, accum_out=z[:])
-        copy_ta(0)
-        xp_pool(0)
+        xp_pool(3)
         nc.scalar.activation(out=px[:], in_=ag[:], func=ACT.Exp, bias=nm[:])
-        xp_vec(2)
-        nc.vector.reciprocal(out=rz[:], in_=z[:])
-        nc.scalar.activation(out=gk[:], in_=fk[:], func=ACT.Copy, scale=rz[:])
+        xp_vec(0)
+        xp_vec(1)
+        for k in range(EARLY):
+            nc.scalar.activation(out=zk[:, NCH + k : NCH + k + 1], in_=zk[:, k : k + 1], func=ACT.Copy, scale=fk[:, k : k + 1])
+        exp_chunk(2, nm[:])
+        copy_ta(0)
         copy_ta(1)
-        xp_pool(1)
-        nc.scalar.activation(out=c1[:], in_=gk[:], func=ACT.Copy, scale=nt[:])
-        copy_ta(2)
         for sl, gr, oc in halves:
             nc.vector.tensor_reduce(out=sg[:, gr], in_=by_group(px[:, sl]), axis=AX.X, op=ALU.add, negate=True)
-        for sl, gr, oc in halves:
-            nc.vector.reciprocal(out=rs[:, gr], in_=sg[:, gr])
-        xq_vec(3)
-        copy_ta(3)
-        for sl, gr, oc in halves:
-            nc.vector.tensor_tensor(out=eg[:, gr], in0=t64[:, gr], in1=rs[:, gr], op=ALU.mult)
+        nc.vector.reciprocal(out=rs[:, halves[0][1]], in_=sg[:, halves[0][1]])
+        nc.vector.tensor_reduce(out=z[:], in_=zk[:, EARLY : NCH + EARLY], axis=AX.X, op=ALU.add)
+        nc.vector.reciprocal(out=rs[:, halves[1][1]], in_=sg[:, halves[1][1]])
+        nc.vector.reciprocal(out=rz[:], in_=z[:])
+        copy_ta(2)
+        nc.scalar.activation(out=gk[:], in_=fk[:], func=ACT.Copy, scale=rz[:])
+        nc.vector.tensor_tensor(out=eg[:, halves[0][1]], in0=t64[:, halves[0][1]], in1=rs[:, halves[0][1]], op=ALU.mult)
+        nc.vector.tensor_scalar(out=c1[:], in0=fk[:], scalar1=rz[:], scalar2=nt[:], op0=ALU.mult, op1=ALU.mult)
+        nc.vector.tensor_tensor(out=eg[:, halves[1][1]], in0=t64[:, halves[1][1]], in1=rs[:, halves[1][1]], op=ALU.mult)
         for sl, gr, oc in halves:
             nc.vector.tensor_tensor(out=by_group(w[:, sl]), in0=by_group(px[:, sl]), in1=spread(eg[:, gr]), op=ALU.mult)
+        xq_vec(2)
         HS, HG, HO = I // 2, G // 2, I // 32
         halves = [(slice(h * HS, (h + 1) * HS), slice(h * HG, (h + 1) * HG), slice(h * HO, (h + 1) * HO)) for h in range(2)]
         for sl, gr, oc in halves:
@@ -192,8 +205,8 @@ def tile_attend_hvgroupshare_heads_kernel(tc, hid, voc_words, voc_scales, target
         pq = [sb.tile([P, CH], F32, name="pq%d" % k) for k in range(NCH)]
         mid = [sb.tile([P, CH], F32, name="mid%d" % k) for k in range(NCH)]
         res = [sb.tile([P, CH], F32, name="res%d" % k) for k in range(NCH)]
-        s_ps = [ps.tile([P, CH], F32, name="s_ps%d" % k, tag="lo%d" % k) for k in range(NCH)]
-        r_ps = [ps.tile([P, CH], F32, name="r_ps%d" % k, tag="hi%d" % k) for k in range(NCH)]
+        s_ps = [ps.tile([P, CH], F32, name="s_ps%d" % k, tag="hi%d" % k) for k in range(NCH)]
+        r_ps = [ps.tile([P, CH], F32, name="r_ps%d" % k, tag="lo%d" % ((k + 1) % NCH)) for k in range(NCH)]
 
         def turn(bank, src, first, last):
             for b in range(NB):
@@ -203,9 +216,9 @@ def tile_attend_hvgroupshare_heads_kernel(tc, hid, voc_words, voc_scales, target
 
         for k in range(NCH):
             turn(s_ps[k], base_sb[k], True, False)
-        for k in (3,):
+        for k in (2,):
             turn(s_ps[k], xq[k], False, False)
-        for k in (2, 0, 1):
+        for k in (0, 1, 3):
             nc.scalar.activation(out=xq[k][:], in_=xp[k][:], func=ACT.Copy, scale=c1[:, k : k + 1], accum_out=yk[:, k : k + 1])
             turn(s_ps[k], xq[k], False, False)
         nc.scalar.activation(out=ny[:], in_=yk[:], func=ACT.Copy, scale=-1.0, accum_out=mu[:])

from contextlib import ExitStack

import concourse.mybir as mybir
from concourse.masks import make_identity

D, V, Q, I, G = 512, 2048, 128, 512, 64
FLOPS = 2 * 2 * D * Q * V

F32 = mybir.dt.float32
BF16 = mybir.dt.bfloat16
I32 = mybir.dt.int32
U32 = mybir.dt.uint32
U16 = mybir.dt.uint16
U8 = mybir.dt.uint8
FP8X4 = mybir.dt.float8_e4m3fn_x4
ALU = mybir.AluOpType
ACT = mybir.ActivationFunctionType
AX = mybir.AxisListType

P = 128
PACK = 4
CH = 512
NCH = V // CH
GS = I // G
NB = CH // P
EARLY = 2


def tile_attend_hvgroupshare_heads_kernel(tc, hid, voc_words, voc_scales, target, dhid, base, offs, out):
    nc = tc.nc
    with ExitStack() as ctx:
        sb = ctx.enter_context(tc.tile_pool(name="sb", bufs=1))
        ps = ctx.enter_context(tc.psum_pool(name="ps", bufs=1))

        offsets = sb.tile([P, I // 16], U16, name="offsets")
        vsc = sb.tile([P, CH], U8, name="vsc", align_bytes=64)
        words = [sb.tile([P, CH], U32, name="words%d" % k, align_bytes=64) for k in range(NCH)]
        raw = [sb.tile([P, PACK, Q], F32, name="raw%d" % j) for j in range(2)]
        grouped = [sb.tile([P, Q, PACK], BF16, name="grouped%d" % j, tag="grouped%d" % j, align_bytes=64) for j in range(2)]
        codes = [sb.tile([P, Q], U32, name="codes%d" % j, align_bytes=64) for j in range(2)]
        hsc = [sb.tile([P, Q], U8, name="hsc%d" % j, align_bytes=64) for j in range(2)]
        tgt = sb.tile([P, G], F32, name="tgt")
        base_sb = [sb.tile([P, CH], F32, name="base%d" % k) for k in range(NCH)]
        ta_sb = sb.tile([P, V], F32, name="ta_sb")
        xs = sb.tile([P, V], F32, name="xs")
        ident = sb.tile([P, P], F32, name="ident")

        nc.vector.memset(vsc[:].bitcast(I32), 0)
        nc.vector.memset(xs[:], 0.0)
        make_identity(nc, ident[:])

        scale_rows = voc_scales[0].bitcast(I32).rearrange("r (j c) -> j r c", j=NCH)
        word_rows = voc_words[0].rearrange("p n t -> p (n t)").bitcast(I32)
        def load_scales(qd, queue):
            queue.dma_start(out=vsc[32 * qd : 32 * qd + 16, :].bitcast(I32), in_=scale_rows[:, 4 * qd : 4 * qd + 4, :])

        def load_words(k, queue=nc.sync):
            queue.dma_start(out=words[k][:].bitcast(I32), in_=word_rows[:, k * CH : (k + 1) * CH])

        nc.sync.dma_start(out=raw[0][:], in_=hid.rearrange("(p j) w -> p j w", j=PACK))
        load_scales(2, nc.scalar)
        load_words(0)
        load_scales(3, nc.scalar)
        load_scales(0, nc.sync)
        load_scales(1, nc.sync)
        nc.sync.dma_start(out=raw[1][:], in_=dhid.rearrange("(p j) w -> p j w", j=PACK))
        load_words(1)
        load_words(2)
        load_words(3)
        nc.sync.dma_start(offsets[:], offs)
        nc.sync.dma_start(out=tgt[:], in_=target)
        for k in range(NCH):
            nc.sync.dma_start(out=base_sb[k][:], in_=base[:, k * CH : (k + 1) * CH])

        for j in range(2):
            nc.vector.tensor_copy(out=grouped[j][:], in_=raw[j][:].rearrange("p j w -> p w j"))
            nc.vector.quantize_mx(out=codes[j][:].bitcast(FP8X4), scales=hsc[j][:], in_=grouped[j][:].rearrange("p w j -> p (w j)"))

        def scores(j, k, bank):
            nc.tensor.matmul_mx(out=bank[:], lhsT=codes[j][:].bitcast(FP8X4), lhsT_scale=hsc[j][:],
                                rhs=words[k][:].bitcast(FP8X4), rhs_scale=vsc[4 * k : P, :], start=True, stop=True)

        def cols(k):
            return slice(k * CH, (k + 1) * CH)

        a_ps = [ps.tile([P, CH], F32, name="a_ps%d" % k, tag="lo%d" % k) for k in range(NCH)]
        for k in range(NCH):
            scores(0, k, a_ps[k])

        a_sb = sb.tile([P, V], F32, name="a_sb", tag="grouped1", align_bytes=64)
        mk = sb.tile([P, NCH], F32, name="mk")
        nmk = sb.tile([P, EARLY], F32, name="nmk")
        nm = sb.tile([P, 1], F32, name="nm")
        fk = sb.tile([P, NCH], F32, name="fk")
        zk = sb.tile([P, NCH + EARLY], F32, name="zk")
        yk = sb.tile([P, NCH], F32, name="yk")
        p_sb = [sb.tile([P, CH], F32, name="p%d" % k) for k in range(NCH)]
        xp = [sb.tile([P, CH], F32, name="xp%d" % k) for k in range(NCH)]
        t64 = sb.tile([P, G], F32, name="t64")
        nt = sb.tile([P, 1], F32, name="nt")
        ag = sb.tile([P, I], F32, name="ag")
        px = sb.tile([P, I], F32, name="px")
        nc.gpsimd.memset(fk[:], 1.0)

        def exp_chunk(k, shift):
            nc.scalar.activation(out=p_sb[k][:], in_=a_sb[:, cols(k)], func=ACT.Exp, bias=shift, accum_out=zk[:, k : k + 1])

        def copy_ta(k):
            nc.scalar.copy(out=ta_sb[:, cols(k)], in_=t_ps[k][:])

        for k in range(NCH):
            nc.vector.tensor_scalar(out=a_sb[:, cols(k)], in0=a_ps[k][:], scalar1=1.0, scalar2=None, op0=ALU.mult, op1=ALU.max,
                                    accum_out=mk[:, k : k + 1])
            if k < EARLY:
                nc.scalar.activation(out=nmk[:, k : k + 1], in_=mk[:, k : k + 1], func=ACT.Copy, scale=-1.0)
                exp_chunk(k, nmk[:, k : k + 1])
        nc.vector.tensor_reduce(out=nm[:], in_=mk[:], axis=AX.X, op=ALU.max, negate=True)
        t_ps = {}

        def tangent(k, tag):
            t_ps[k] = ps.tile([P, CH], F32, name="t_ps%d" % k, tag=tag)
            scores(1, k, t_ps[k])

        tangent(3, "lo0")
        tangent(0, "lo2")
        tangent(1, "lo3")
        nc.scalar.activation(out=t64[:], in_=tgt[:], func=ACT.Copy, scale=-64.0, accum_out=nt[:])
        copy_ta(3)
        tangent(2, "lo0")
        nc.vector.tensor_copy(out=ag[:], in_=a_sb[:].indirect(offsets[:]))
        nc.scalar.activation(out=fk[:, 0:EARLY], in_=mk[:, 0:EARLY], func=ACT.Exp, bias=nm[:])
        exp_chunk(3, nm[:])

        z = sb.tile([P, 1], F32, name="z")
        rz = sb.tile([P, 1], F32, name="rz")
        gk = sb.tile([P, NCH], F32, name="gk")
        c1 = sb.tile([P, NCH], F32, name="c1")
        ny = sb.tile([P, NCH], F32, name="ny")
        mu = sb.tile([P, 1], F32, name="mu")
        c2 = sb.tile([P, NCH], F32, name="c2")
        sg = sb.tile([P, G], F32, name="sg")
        rs = sb.tile([P, G], F32, name="rs")
        eg = sb.tile([P, G], F32, name="eg")
        w = sb.tile([P, I], F32, name="w")
        xw = sb.tile([P, I], F32, name="xw")
        nx = sb.tile([P, G], F32, name="nx")
        kg = sb.tile([P, G], F32, name="kg")
        pk = sb.tile([P, I], F32, name="pk")

        def by_group(ap):
            return ap.rearrange("p (g s) -> p g s", s=GS)

        def spread(ap):
            return ap.unsqueeze(2).to_broadcast([P, ap.shape[1], GS])

        def xp_pool(k):
            nc.gpsimd.tensor_tensor(out=xp[k][:], in0=ta_sb[:, cols(k)], in1=p_sb[k][:], op=ALU.mult)

        xq = [sb.tile([P, CH], F32, name="xq%d" % k) for k in range(NCH)]

        def xq_vec(k):
            nc.vector.scalar_tensor_tensor(out=xq[k][:], in0=t_ps[k][:], scalar=c1[:, k : k + 1], in1=p_sb[k][:], op0=ALU.mult, op1=ALU.mult,
                                           accum_out=yk[:, k : k + 1])

        def xp_vec(k):
            nc.vector.tensor_tensor(out=xp[k][:], in0=t_ps[k][:], in1=p_sb[k][:], op=ALU.mult)

        HS, HG, HO = I // 2, G // 2, I // 32
        halves = [(slice(h * HS, (h + 1) * HS), slice(h * HG, (h + 1) * HG), slice(h * HO, (h + 1) * HO)) for h in range(2)]
        xp_pool(3)
        nc.scalar.activation(out=px[:], in_=ag[:], func=ACT.Exp, bias=nm[:])
        xp_vec(0)
        xp_vec(1)
        for k in range(EARLY):
            nc.scalar.activation(out=zk[:, NCH + k : NCH + k + 1], in_=zk[:, k : k + 1], func=ACT.Copy, scale=fk[:, k : k + 1])
        exp_chunk(2, nm[:])
        copy_ta(0)
        copy_ta(1)
        for sl, gr, oc in halves:
            nc.vector.tensor_reduce(out=sg[:, gr], in_=by_group(px[:, sl]), axis=AX.X, op=ALU.add, negate=True)
        nc.vector.reciprocal(out=rs[:, halves[0][1]], in_=sg[:, halves[0][1]])
        nc.vector.tensor_reduce(out=z[:], in_=zk[:, EARLY : NCH + EARLY], axis=AX.X, op=ALU.add)
        nc.vector.reciprocal(out=rs[:, halves[1][1]], in_=sg[:, halves[1][1]])
        nc.vector.reciprocal(out=rz[:], in_=z[:])
        copy_ta(2)
        nc.scalar.activation(out=gk[:], in_=fk[:], func=ACT.Copy, scale=rz[:])
        nc.vector.tensor_tensor(out=eg[:, halves[0][1]], in0=t64[:, halves[0][1]], in1=rs[:, halves[0][1]], op=ALU.mult)
        nc.vector.tensor_scalar(out=c1[:], in0=fk[:], scalar1=rz[:], scalar2=nt[:], op0=ALU.mult, op1=ALU.mult)
        nc.vector.tensor_tensor(out=eg[:, halves[1][1]], in0=t64[:, halves[1][1]], in1=rs[:, halves[1][1]], op=ALU.mult)
        for sl, gr, oc in halves:
            nc.vector.tensor_tensor(out=by_group(w[:, sl]), in0=by_group(px[:, sl]), in1=spread(eg[:, gr]), op=ALU.mult)
        xq_vec(2)
        HS, HG, HO = I // 2, G // 2, I // 32
        halves = [(slice(h * HS, (h + 1) * HS), slice(h * HG, (h + 1) * HG), slice(h * HO, (h + 1) * HO)) for h in range(2)]
        for sl, gr, oc in halves:
            nc.vector.tensor_tensor(out=xw[:, sl], in0=ta_sb[:].indirect(offsets[:, oc]), in1=w[:, sl], op=ALU.mult)
        for sl, gr, oc in halves:
            nc.vector.tensor_reduce(out=nx[:, gr], in_=by_group(xw[:, sl]), axis=AX.X, op=ALU.add)
        for sl, gr, oc in halves:
            nc.vector.tensor_tensor(out=kg[:, gr], in0=nx[:, gr], in1=rs[:, gr], op=ALU.mult)
        for sl, gr, oc in halves:
            nc.vector.tensor_tensor(out=by_group(pk[:, sl]), in0=by_group(px[:, sl]), in1=spread(kg[:, gr]), op=ALU.mult)
        nc.vector.tensor_tensor(out=xs[:].indirect(offsets[:]), in0=xw[:], in1=pk[:], op=ALU.add)

        pq = [sb.tile([P, CH], F32, name="pq%d" % k) for k in range(NCH)]
        mid = [sb.tile([P, CH], F32, name="mid%d" % k) for k in range(NCH)]
        res = [sb.tile([P, CH], F32, name="res%d" % k) for k in range(NCH)]
        s_ps = [ps.tile([P, CH], F32, name="s_ps%d" % k, tag="hi%d" % k) for k in range(NCH)]
        r_ps = [ps.tile([P, CH], F32, name="r_ps%d" % k, tag="lo%d" % ((k + 1) % NCH)) for k in range(NCH)]

        def turn(bank, src, first, last):
            for b in range(NB):
                blk = slice(b * P, (b + 1) * P)
                nc.tensor.matmul(out=bank[:, blk], lhsT=src[:, blk], rhs=ident[:], is_transpose=True,
                                 start=(first and b == 0), stop=(last and b == NB - 1))

        for k in range(NCH):
            turn(s_ps[k], base_sb[k], True, False)
        for k in (2,):
            turn(s_ps[k], xq[k], False, False)
        for k in (0, 1, 3):
            nc.scalar.activation(out=xq[k][:], in_=xp[k][:], func=ACT.Copy, scale=c1[:, k : k + 1], accum_out=yk[:, k : k + 1])
            turn(s_ps[k], xq[k], False, False)
        nc.scalar.activation(out=ny[:], in_=yk[:], func=ACT.Copy, scale=-1.0, accum_out=mu[:])
        nc.scalar.activation(out=c2[:], in_=gk[:], func=ACT.Copy, scale=mu[:])
        for k in range(NCH + 2):
            if k < NCH:
                nc.scalar.activation(out=pq[k][:], in_=p_sb[k][:], func=ACT.Copy, scale=c2[:, k : k + 1])
                turn(s_ps[k], pq[k], False, True)
            if k > 1:
                nc.scalar.copy(out=mid[k - 2][:], in_=s_ps[k - 2][:])
                turn(r_ps[k - 2], mid[k - 2], True, True)
        c0 = 0
        for width in (256, 256, 512, 512, 512):
            k, lo = divmod(c0, CH)
            nc.vector.tensor_tensor(out=res[k][:, lo : lo + width], in0=r_ps[k][:, lo : lo + width], in1=xs[:, c0 : c0 + width], op=ALU.add)
            nc.sync.dma_start(out=out[:, c0 : c0 + width], in_=res[k][:, lo : lo + width])
            c0 = c0 + width
